import numpy as np
import ml_dtypes


def mxq(x, axis, fmt="e4m3"):
    dtype, down = {"e4m3": (ml_dtypes.float8_e4m3fn, 7), "e5m2": (ml_dtypes.float8_e5m2, 14)}[fmt]
    v = np.moveaxis(np.asarray(x, np.float32).astype(ml_dtypes.bfloat16).astype(np.float64), axis, -1)
    blocks = v.reshape(v.shape[:-1] + (-1, 32))
    amax = np.abs(blocks).max(-1, keepdims=True)
    byte = np.maximum(np.where(amax > 0, np.frexp(amax)[1] - 1 + 127, 0) - down, 1)
    scale = np.exp2(byte - 127.0)
    codes = (blocks / scale).astype(np.float32).astype(dtype).astype(np.float64)
    return np.moveaxis((codes * scale).reshape(v.shape), -1, axis)


WIDE = False


def mx_kscale(k):
    if not WIDE:
        return np.ones(k)
    levels = np.array([10, -10, 5, -5, 0])
    if k % 512:
        return np.exp2(np.random.permutation(np.resize(levels, k // 32))).repeat(32)
    a = np.empty((k // 512, 16))
    for p in range(k // 512):
        a[p, :8] = np.random.permutation(np.resize(levels, 8))
        for g in range(8):
            far = levels[np.abs(levels - a[p, g]) >= 10]
            a[p, g + 8] = far[np.random.randint(len(far))]
    return np.exp2(a.ravel()).repeat(32)


BF16 = ml_dtypes.bfloat16


def bf(x):
    return np.asarray(x, np.float32).astype(BF16)


def f64(x):
    return np.asarray(x).astype(np.float64)


D, F, N = 1024, 1024, 512

ALPHA = 0.5


def draw0():
    s = mx_kscale(N)
    t = mx_kscale(N)
    c = 1.0 / np.sqrt(N)
    return {
        "w0": bf(np.random.standard_normal((D, F)) * 0.5),
        "coef": bf(np.random.standard_normal((N, N)) * c * s[None, :]),
        "g": bf((1.0 + 0.1 * np.random.standard_normal(N)) * t),
        "uc": bf(np.random.standard_normal((D, N)) * c / t[None, :]),
        "us": bf(np.random.standard_normal((D, N)) * c / t[None, :]),
        "vc": bf(np.random.standard_normal((N, F)) / s[:, None]),
        "vs": bf(np.random.standard_normal((N, F)) / s[:, None]),
    }


def core(w0, coef, g, uc, us, vc, vs):
    cq = mxq(f64(coef), 1, "e4m3")
    rc = cq @ mxq(f64(vc), 0, "e4m3")
    rs = cq @ mxq(f64(vs), 0, "e4m3")
    gain = f64(g)[:, None]
    zc = gain * rc
    zs = gain * rs
    pc = mxq(f64(uc), 1, "e4m3") @ mxq(zc, 0, "e4m3")
    ps = mxq(f64(us), 1, "e4m3") @ mxq(zs, 0, "e4m3")
    return f64(w0) + ALPHA * (pc - ps)


def e4m3fn_bytes(y):
    return np.clip(np.asarray(y, np.float64), -448.0, 448.0).astype(np.float32).astype(ml_dtypes.float8_e4m3fn).view(np.uint8)


def e4m3fn_values(b):
    return np.asarray(b, np.uint8).view(ml_dtypes.float8_e4m3fn).astype(np.float64)


def setup_inputs():
    d = draw0()
    x0 = np.asarray(d['vs']).astype(np.float64)
    s = (np.max(np.abs(x0), axis=(1,), keepdims=True) / 448.0).astype(np.float32)
    out = {}
    for k, v in d.items():
        if k == 'vs':
            out['vs_bytes'] = e4m3fn_bytes(x0 / s.astype(np.float64))
            out['vs_scale'] = s
        else:
            out[k] = v
    return out


def reference(w0, coef, g, uc, us, vc, vs_bytes, vs_scale):
    return core(w0, coef, g, uc, us, vc, e4m3fn_values(vs_bytes) * vs_scale.astype(np.float64))

@@ -1,0 +1,335 @@
+from contextlib import ExitStack
+
+import concourse.mybir as mybir
+from concourse.masks import make_identity
+
+D, F, N = 1024, 1024, 512
+FLOPS = 2 * 2 * N * N * F + 2 * 2 * D * N * F
+
+F32 = mybir.dt.float32
+BF16 = mybir.dt.bfloat16
+U32 = mybir.dt.uint32
+U8 = mybir.dt.uint8
+FP8 = mybir.dt.float8_e4m3fn
+FP8X4 = mybir.dt.float8_e4m3fn_x4
+MULT = mybir.AluOpType.mult
+ADD = mybir.AluOpType.add
+COPY = mybir.ActivationFunctionType.Copy
+
+P = 128
+T = 4
+H = 512
+I = 8
+
+
+def tile_fourierftgivenbases_kernel(tc, w0, coef, g, uc, us, vc, vs_bytes, vs_scale, out):
+    nc = tc.nc
+    with ExitStack() as ctx:
+        sb = ctx.enter_context(tc.tile_pool(name="sb", bufs=1))
+        ps = ctx.enter_context(tc.psum_pool(name="ps", bufs=1))
+        ctx.enter_context(tc.manual_schedule())
+
+        def tile(name, shape, dt):
+            return sb.tile(shape, dt, name=name, align_bytes=64)
+
+        def load(name, shape, dt, src):
+            t = tile(name, shape, dt)
+            nc.sync.dma_start(out=t[:], in_=src)
+            return t
+
+        vsb_v = vs_bytes.rearrange("(p t) f -> p t f", t=T)
+        vc_v = vc.rearrange("(p t) f -> p t f", t=T)
+        coef_v = coef.rearrange("(p t) k -> p t k", t=T)
+        u_v = {"c": uc.rearrange("(p i) n -> p i n", i=I), "s": us.rearrange("(p i) n -> p i n", i=I)}
+        w0_v = w0.rearrange("(p i) f -> p i f", i=I)
+        out_v = out.rearrange("(p i) f -> p i f", i=I)
+
+        vscale = tile("vscale", [P, T], F32)
+        nc.scalar.dma_start(out=vscale[:], in_=vs_scale.rearrange("(p t) o -> p (t o)", t=T))
+        gp = tile("gp", [P, T], BF16)
+        nc.scalar.dma_start(out=gp[:], in_=g.rearrange("(p t) -> p t", t=T))
+
+        vsb = {}
+        vcr = {}
+        u_raw = {}
+        coef_raw = {}
+        w0_sb = {}
+        vsb[0] = load("vsb0", [P, T, H], U8, vsb_v[:, :, 0:H])
+        vsb[1] = load("vsb1", [P, T, H], U8, vsb_v[:, :, H:F])
+        coef_raw[1] = load("coef1", [P, 2, N], BF16, coef_v[:, 2 : 4, :])
+        coef_raw[0] = load("coef0", [P, 2, N], BF16, coef_v[:, 0 : 2, :])
+        vcr[0] = load("vcr0", [P, T, H], BF16, vc_v[:, :, 0:H])
+        u_raw["c", 0] = load("uc0", [P, 4, N], BF16, u_v["c"][:, 0 : 4, :])
+        vcr[1] = load("vcr1", [P, T, H], BF16, vc_v[:, :, H:F])
+        u_raw["s", 1] = load("us1", [P, 4, N], BF16, u_v["s"][:, 4 : 8, :])
+        u_raw["s", 0] = load("us0", [P, 4, N], BF16, u_v["s"][:, 0 : 4, :])
+        w0_sb[0] = load("w0_0", [P, 2, F], BF16, w0_v[:, 0 : 2, :])
+        u_raw["c", 1] = load("uc1", [P, 4, N], BF16, u_v["c"][:, 4 : 8, :])
+        w0_sb[3] = load("w0_3", [P, 2, F], BF16, w0_v[:, 6 : 8, :])
+        w0_sb[2] = load("w0_2", [P, 2, F], BF16, w0_v[:, 4 : 6, :])
+        w0_sb[1] = load("w0_1", [P, 2, F], BF16, w0_v[:, 2 : 4, :])
+        ident_f = tile("ident_f", [P, P], F32)
+        make_identity(nc, ident_f[:])
+        ident_b = tile("ident_b", [P, P], BF16)
+        nc.gpsimd.tensor_copy(out=ident_b[:], in_=ident_f[:])
+
+        def sc_bank(dt, name):
+            return ps.tile([P, 512 if dt == F32 else 1024], dt, name=name, tag="sc", bufs=3)
+
+        def zo_bank(name):
+            return ps.tile([P, 512], F32, name=name, tag="zo", bufs=5)
+
+        codes = {}
+        scales = {}
+        inter = {}
+        sbank = {}
+
+        def new_inter(key, cols=512):
+            inter[key] = tile("in_" + key, [P, cols * T], BF16)
+
+        def quant(key, part=0, parts=1):
+            if key not in codes:
+                codes[key] = tile("co_" + key, [P, 512], U32)
+                scales[key] = tile("sl_" + key, [P, 512], U8)
+            cols = slice(part * 512 // parts, (part + 1) * 512 // parts)
+            ins = slice(part * 2048 // parts, (part + 1) * 2048 // parts)
+            nc.vector.quantize_mx(out=codes[key][:, cols].bitcast(FP8X4), scales=scales[key][:, cols], in_=inter[key][:, ins])
+
+        def mx(dst, lkey, l0, rkey, r0, n, start, stop):
+            nc.tensor.matmul_mx(
+                out=dst,
+                lhsT=codes[lkey][:, l0 : l0 + P].bitcast(FP8X4),
+                lhsT_scale=scales[lkey][:, l0 : l0 + P],
+                rhs=codes[rkey][:, r0 : r0 + n].bitcast(FP8X4),
+                rhs_scale=scales[rkey][:, r0 : r0 + n],
+                start=start,
+                stop=stop,
+            )
+
+        def transposes(raw, first, key, half):
+            bank = sc_bank(F32, "tr_%s%d" % (key, half))
+            sbank[key, half] = bank
+            for i in range(2):
+                words = raw[:, first + i, :].bitcast(F32)
+                for u in range(2):
+                    nc.tensor.transpose(bank[:, (2 * i + u) * P : (2 * i + u + 1) * P], words[:, u::2], ident_f[:])
+
+        def transposes_out(key, half, eng):
+            bank = sbank[key, half]
+            copy = nc.scalar.copy if eng == "s" else nc.vector.tensor_copy
+            dst = inter[key][:].bitcast(F32)[:, half * 512 : (half + 1) * 512]
+            copy(
+                out=dst.rearrange("p (i r u) -> p i r u", i=2, u=2),
+                in_=bank[:].rearrange("p (i u r) -> p i r u", i=2, u=2),
+            )
+
+        def pe_inter(planes, key, half):
+            bank = sc_bank(BF16, "il_%s%d" % (key, half))
+            sbank[key, half] = bank
+            for b in range(2):
+                f0 = half * 256 + b * 128
+                nc.tensor.matmul(
+                    bank[:, b * 512 : (b + 1) * 512],
+                    ident_b[:],
+                    planes[:, :, f0 : f0 + 128].rearrange("p t f -> p f t"),
+                    start=True,
+                    stop=True,
+                )
+
+        def pe_inter_out(key, half, eng):
+            copy = nc.scalar.copy if eng == "s" else nc.vector.tensor_copy
+            copy(out=inter[key][:, half * 1024 : (half + 1) * 1024], in_=sbank[key, half][:])
+
+        def inter_copy(planes, key, half, eng):
+            copy = nc.scalar.copy if eng == "s" else nc.vector.tensor_copy
+            copy(
+                out=inter[key][:, half * 1024 : (half + 1) * 1024].rearrange("p (f t) -> p f t", t=T),
+                in_=planes[:, :, half * 256 : (half + 1) * 256].rearrange("p t f -> p f t"),
+            )
+
+        vsw = {h: tile("vsw%d" % h, [P, T, H], BF16) for h in range(2)}
+
+        def widen(h, t, eng):
+            src = vsb[h][:, t, :].bitcast(FP8)
+            if eng == "v":
+                nc.vector.tensor_scalar(out=vsw[h][:, t, :], in0=src, scalar1=vscale[:, t : t + 1], scalar2=None, op0=MULT)
+            else:
+                nc.scalar.activation(out=vsw[h][:, t, :], in_=src, func=COPY, scale=vscale[:, t : t + 1])
+
+        zbank = {}
+
+        def z_mm(o, h, q):
+            bank = zo_bank("z%s%d%d" % (o, h, q))
+            for t in range(T):
+                mx(bank[:, t * P : (t + 1) * P], "coef", t * P, "v%s%d" % (o, h), q * P, P, True, True)
+            zbank[o, h, q] = bank
+
+        gain = {}
+        zpl = tile("zpl", [P, T, H], BF16)
+
+        def zp_mm(t):
+            bank = zo_bank("zp%d" % t)
+            mx(bank[:], "coef", t * P, "vs1", 0, H, True, True)
+            zbank["p", t] = bank
+
+        def zp_ev(t):
+            nc.scalar.activation(out=zpl[:, t, :], in_=zbank["p", t][:], func=COPY, scale=gneg32[:, t : t + 1])
+
+        def z_ev(o, h, q):
+            nc.vector.tensor_tensor(
+                out=inter["z%s%d" % (o, h)][:, q * 512 : (q + 1) * 512].rearrange("p (n t) -> p n t", t=T),
+                in0=zbank[o, h, q][:].rearrange("p (t n) -> p n t", t=T),
+                in1=gain[o][:].unsqueeze(1).to_broadcast([P, P, T]),
+                op=MULT,
+            )
+
+        obank = {}
+
+        def o_mm(h, i):
+            bank = zo_bank("o%d%d" % (h, i))
+            l0 = (i % 4) * P
+            mx(bank[:], "uc%d" % (i // 4), l0, "zc%d" % h, 0, H, True, False)
+            mx(bank[:], "us%d" % (i // 4), l0, "zs%d" % h, 0, H, False, True)
+            obank[h, i] = bank
+
+        def o_ev(h, i, eng):
+            bank = obank[h, i]
+            w = w0_sb[i // 2][:, i % 2, h * H : (h + 1) * H]
+            o = tile("ot%d%d" % (h, i), [P, H], F32)
+            if eng == "v":
+                nc.vector.scalar_tensor_tensor(out=o[:], in0=bank[:], scalar=0.5, in1=w, op0=MULT, op1=ADD)
+            else:
+                half = tile("oh%d%d" % (h, i), [P, H], F32)
+                nc.scalar.activation(out=half[:], in_=bank[:], func=COPY, scale=0.5)
+                nc.gpsimd.tensor_tensor(out=o[:], in0=half[:], in1=w, op=ADD)
+            nc.sync.dma_start(out=out_v[:, i, h * H : (h + 1) * H], in_=o[:])
+
+        for k in ("coef", "vc0", "vc1", "vs0", "vs1", "zc0", "zc1", "zs0", "zs1", "uc0", "uc1", "us0", "us1"):
+            new_inter(k)
+
+        gneg = tile("gneg", [P, T], BF16)
+        nc.gpsimd.tensor_scalar(out=gneg[:], in0=gp[:], scalar1=-1.0, scalar2=None, op0=MULT)
+        gneg32 = tile("gneg32", [P, T], F32)
+        nc.gpsimd.tensor_scalar(out=gneg32[:], in0=gp[:], scalar1=-1.0, scalar2=None, op0=MULT)
+        gain["c"] = gp
+        gain["s"] = gneg
+
+        widen(0, 0, "s")
+        widen(0, 1, "v")
+        widen(1, 0, "v")
+        widen(0, 2, "s")
+        widen(1, 2, "v")
+        transposes(coef_raw[1], 0, "coef", 1)
+        transposes(coef_raw[0], 0, "coef", 0)
+        widen(0, 3, "v")
+        widen(1, 1, "s")
+        widen(1, 3, "v")
+        inter_copy(vsw[0], "vs0", 1, "s")
+        pe_inter(vcr[0], "vc0", 1)
+        transposes_out("coef", 1, "s")
+        pe_inter(vsw[1], "vs1", 0)
+        transposes_out("coef", 0, "s")
+        transposes(u_raw["c", 0], 0, "uc0", 0)
+        inter_copy(vsw[0], "vs0", 0, "v")
+        inter_copy(vsw[1], "vs1", 1, "v")
+        inter_copy(vcr[0], "vc0", 0, "v")
+        quant("vs0", 0, 2)
+        pe_inter_out("vc0", 1, "s")
+        pe_inter_out("vs1", 0, "s")
+        quant("vs0", 1, 2)
+        transposes_out("uc0", 0, "s")
+        quant("coef")
+        quant("vc0")
+        quant("vs1")
+        transposes(u_raw["c", 0], 2, "uc0", 1)
+        inter_copy(vcr[1], "vc1", 1, "s")
+        z_mm("s", 0, 0)
+        z_ev("s", 0, 0)
+        z_mm("c", 0, 3)
+        z_ev("c", 0, 3)
+        inter_copy(vcr[1], "vc1", 0, "s")
+        z_mm("s", 0, 1)
+        z_mm("c", 0, 2)
+        z_ev("s", 0, 1)
+        transposes_out("uc0", 1, "s")
+        z_mm("s", 0, 2)
+        z_mm("s", 0, 3)
+        z_ev("c", 0, 2)
+        z_ev("s", 0, 3)
+        transposes(u_raw["s", 0], 0, "us0", 0)
+        transposes_out("us0", 0, "s")
+        transposes(u_raw["s", 0], 2, "us0", 1)
+        z_ev("s", 0, 2)
+        quant("vc1")
+        quant("uc0")
+        z_mm("c", 0, 0)
+        z_ev("c", 0, 0)
+        zp_mm(2)
+        transposes_out("us0", 1, "s")
+        z_mm("c", 0, 1)
+        z_ev("c", 0, 1)
+        zp_mm(3)
+        quant("zs0")
+        quant("us0")
+        zp_mm(1)
+        transposes(u_raw["s", 1], 0, "us1", 0)
+        quant("zc0")
+        transposes(u_raw["s", 1], 2, "us1", 1)
+        zp_ev(2)
+        transposes(u_raw["c", 1], 0, "uc1", 0)
+        zp_ev(3)
+        transposes_out("us1", 0, "s")
+        transposes(u_raw["c", 1], 2, "uc1", 1)
+        zp_mm(0)
+        z_mm("c", 1, 1)
+        z_mm("c", 1, 0)
+        zp_ev(1)
+        z_mm("c", 1, 2)
+        transposes_out("us1", 1, "s")
+        quant("us1")
+        transposes_out("uc1", 1, "s")
+        zp_ev(0)
+        z_ev("c", 1, 0)
+        z_ev("c", 1, 1)
+        z_ev("c", 1, 2)
+        o_mm(0, 2)
+        pe_inter(zpl, "zs1", 1)
+        transposes_out("uc1", 0, "s")
+        o_ev(0, 2, "s")
+        o_mm(0, 3)
+        o_mm(0, 1)
+        quant("uc1")
+        z_mm("c", 1, 3)
+        pe_inter_out("zs1", 1, "s")
+        o_ev(0, 1, "v")
+        o_mm(0, 0)
+        o_ev(0, 3, "s")
+        o_mm(0, 6)
+        z_ev("c", 1, 3)
+        o_mm(0, 4)
+        o_mm(0, 7)
+        o_ev(0, 0, "v")
+        quant("zc1")
+        o_ev(0, 4, "v")
+        inter_copy(zpl, "zs1", 0, "s")
+        o_mm(0, 5)
+        quant("zs1")
+        o_mm(1, 5)
+        o_ev(0, 6, "s")
+        o_ev(0, 7, "v")
+        o_ev(0, 5, "v")
+        o_ev(1, 5, "v")
+        o_mm(1, 4)
+        o_ev(1, 4, "v")
+        o_mm(1, 6)
+        o_mm(1, 0)
+        o_ev(1, 6, "v")
+        o_mm(1, 1)
+        o_ev(1, 0, "v")
+        o_mm(1, 3)
+        o_ev(1, 1, "v")
+        o_mm(1, 2)
+        o_ev(1, 3, "v")
+        o_ev(1, 2, "v")
+        o_mm(1, 7)
+        o_ev(1, 7, "v")

@@ -20,6 +20,7 @@ P = 128
 T = 4
 H = 512
 I = 8
+NDUMMY = 8
 
 
 def tile_fourierftgivenbases_kernel(tc, w0, coef, g, uc, us, vc, vs_bytes, vs_scale, out):
@@ -50,24 +51,24 @@ def tile_fourierftgivenbases_kernel(tc, w0, coef, g, uc, us, vc, vs_bytes, vs_sc
         nc.scalar.dma_start(out=gp[:], in_=g.rearrange("(p t) -> p t", t=T))
 
         vsb = {}
-        vcr = {}
+        vcr = tile("vcr", [P, T, F], BF16)
         u_raw = {}
         coef_raw = {}
         w0_sb = {}
-        vsb[0] = load("vsb0", [P, T, H], U8, vsb_v[:, :, 0:H])
-        vsb[1] = load("vsb1", [P, T, H], U8, vsb_v[:, :, H:F])
-        coef_raw[1] = load("coef1", [P, 2, N], BF16, coef_v[:, 2 : 4, :])
+        vsb[1] = load("vsb1", [P, 2, F], U8, vsb_v[:, 2 : 4, :])
+        vsb[0] = load("vsb0", [P, 2, F], U8, vsb_v[:, 0 : 2, :])
         coef_raw[0] = load("coef0", [P, 2, N], BF16, coef_v[:, 0 : 2, :])
-        vcr[0] = load("vcr0", [P, T, H], BF16, vc_v[:, :, 0:H])
-        u_raw["c", 0] = load("uc0", [P, 4, N], BF16, u_v["c"][:, 0 : 4, :])
-        vcr[1] = load("vcr1", [P, T, H], BF16, vc_v[:, :, H:F])
-        u_raw["s", 1] = load("us1", [P, 4, N], BF16, u_v["s"][:, 4 : 8, :])
-        u_raw["s", 0] = load("us0", [P, 4, N], BF16, u_v["s"][:, 0 : 4, :])
+        coef_raw[1] = load("coef1", [P, 2, N], BF16, coef_v[:, 2 : 4, :])
+        nc.sync.dma_start(out=vcr[:, 0 : 2, :], in_=vc_v[:, 0 : 2, :])
+        nc.sync.dma_start(out=vcr[:, 2 : 4, :], in_=vc_v[:, 2 : 4, :])
         w0_sb[0] = load("w0_0", [P, 2, F], BF16, w0_v[:, 0 : 2, :])
+        u_raw["c", 0] = load("uc0", [P, 4, N], BF16, u_v["c"][:, 0 : 4, :])
+        u_raw["s", 0] = load("us0", [P, 4, N], BF16, u_v["s"][:, 0 : 4, :])
+        w0_sb[1] = load("w0_1", [P, 2, F], BF16, w0_v[:, 2 : 4, :])
         u_raw["c", 1] = load("uc1", [P, 4, N], BF16, u_v["c"][:, 4 : 8, :])
         w0_sb[3] = load("w0_3", [P, 2, F], BF16, w0_v[:, 6 : 8, :])
+        u_raw["s", 1] = load("us1", [P, 4, N], BF16, u_v["s"][:, 4 : 8, :])
         w0_sb[2] = load("w0_2", [P, 2, F], BF16, w0_v[:, 4 : 6, :])
-        w0_sb[1] = load("w0_1", [P, 2, F], BF16, w0_v[:, 2 : 4, :])
         ident_f = tile("ident_f", [P, P], F32)
         make_identity(nc, ident_f[:])
         ident_b = tile("ident_b", [P, P], BF16)
@@ -106,7 +107,8 @@ def tile_fourierftgivenbases_kernel(tc, w0, coef, g, uc, us, vc, vs_bytes, vs_sc
                 stop=stop,
             )
 
-        def transposes(raw, first, key, half):
+        def transposes(key, half):
+            raw, first = (coef_raw[half], 0) if key == "coef" else (u_raw[key[1], int(key[2])], 2 * half)
             bank = sc_bank(F32, "tr_%s%d" % (key, half))
             sbank[key, half] = bank
             for i in range(2):
@@ -123,7 +125,14 @@ def tile_fourierftgivenbases_kernel(tc, w0, coef, g, uc, us, vc, vs_bytes, vs_sc
                 in_=bank[:].rearrange("p (i u r) -> p i r u", i=2, u=2),
             )
 
-        def pe_inter(planes, key, half):
+        def planes_of(key):
+            if key == "zs1":
+                return zpl
+            h = int(key[2])
+            return (vsw if key[1] == "s" else vcr)[:, :, h * H : (h + 1) * H]
+
+        def pe_inter(key, half):
+            planes = planes_of(key)
             bank = sc_bank(BF16, "il_%s%d" % (key, half))
             sbank[key, half] = bank
             for b in range(2):
@@ -140,21 +149,22 @@ def tile_fourierftgivenbases_kernel(tc, w0, coef, g, uc, us, vc, vs_bytes, vs_sc
             copy = nc.scalar.copy if eng == "s" else nc.vector.tensor_copy
             copy(out=inter[key][:, half * 1024 : (half + 1) * 1024], in_=sbank[key, half][:])
 
-        def inter_copy(planes, key, half, eng):
+        def inter_copy(key, half, eng):
+            planes = planes_of(key)
             copy = nc.scalar.copy if eng == "s" else nc.vector.tensor_copy
             copy(
-                out=inter[key][:, half * 1024 : (half + 1) * 1024].rearrange("p (f t) -> p f t", t=T),
-                in_=planes[:, :, half * 256 : (half + 1) * 256].rearrange("p t f -> p f t"),
+                out=inter[key][:, half * 1024 : (half + 1) * 1024].rearrange("p (c i t) -> p c t i", t=T, i=4),
+                in_=planes[:, :, half * 256 : (half + 1) * 256].rearrange("p t (c i) -> p c t i", i=4),
             )
 
-        vsw = {h: tile("vsw%d" % h, [P, T, H], BF16) for h in range(2)}
+        vsw = tile("vsw", [P, T, F], BF16)
 
-        def widen(h, t, eng):
-            src = vsb[h][:, t, :].bitcast(FP8)
+        def widen(t, eng):
+            src = vsb[t // 2][:, t % 2, :].bitcast(FP8)
             if eng == "v":
-                nc.vector.tensor_scalar(out=vsw[h][:, t, :], in0=src, scalar1=vscale[:, t : t + 1], scalar2=None, op0=MULT)
+                nc.vector.tensor_scalar(out=vsw[:, t, :], in0=src, scalar1=vscale[:, t : t + 1], scalar2=None, op0=MULT)
             else:
-                nc.scalar.activation(out=vsw[h][:, t, :], in_=src, func=COPY, scale=vscale[:, t : t + 1])
+                nc.scalar.activation(out=vsw[:, t, :], in_=src, func=COPY, scale=vscale[:, t : t + 1])
 
         zbank = {}
 
@@ -183,6 +193,27 @@ def tile_fourierftgivenbases_kernel(tc, w0, coef, g, uc, us, vc, vs_bytes, vs_sc
                 op=MULT,
             )
 
+        def o2_mm(c, j):
+            bank = zo_bank("q%d%d" % (c, j))
+            for e in range(2):
+                l0 = ((2 * j + e) % 4) * P
+                mx(bank[:, e * 256 : (e + 1) * 256], "uc%d" % (j // 2), l0, "zc1", c * 256, 256, True, False)
+                mx(bank[:, e * 256 : (e + 1) * 256], "us%d" % (j // 2), l0, "zs1", c * 256, 256, False, True)
+            obank["ab"[c], j] = bank
+
+        def o2_ev(c, j, eng):
+            bank = obank["ab"[c], j][:].rearrange("p (e f) -> p e f", e=2)
+            f0 = H + c * 256
+            w = w0_sb[j][:, :, f0 : f0 + 256]
+            o = tile("ou%d%d" % (c, j), [P, 2, 256], F32)
+            if eng == "v":
+                nc.vector.scalar_tensor_tensor(out=o[:], in0=bank, scalar=0.5, in1=w, op0=MULT, op1=ADD)
+            else:
+                half = tile("og%d%d" % (c, j), [P, 2, 256], F32)
+                nc.scalar.activation(out=half[:], in_=bank, func=COPY, scale=0.5)
+                nc.gpsimd.tensor_tensor(out=o[:], in0=half[:], in1=w, op=ADD)
+            nc.sync.dma_start(out=out_v[:, 2 * j : 2 * j + 2, f0 : f0 + 256], in_=o[:])
+
         obank = {}
 
         def o_mm(h, i):
@@ -204,6 +235,12 @@ def tile_fourierftgivenbases_kernel(tc, w0, coef, g, uc, us, vc, vs_bytes, vs_sc
                 nc.gpsimd.tensor_tensor(out=o[:], in0=half[:], in1=w, op=ADD)
             nc.sync.dma_start(out=out_v[:, i, h * H : (h + 1) * H], in_=o[:])
 
+        wz = tile("wz", [P, 512], BF16)
+        nc.vector.memset(wz[:], 0.0)
+        for j in range(NDUMMY):
+            wb = sc_bank(F32, "warm%d" % j)
+            nc.tensor.matmul(wb[:], wz[:, 0:P], wz[:], start=True, stop=True)
+
         for k in ("coef", "vc0", "vc1", "vs0", "vs1", "zc0", "zc1", "zs0", "zs1", "uc0", "uc1", "us0", "us1"):
             new_inter(k)
 
@@ -214,122 +251,119 @@ def tile_fourierftgivenbases_kernel(tc, w0, coef, g, uc, us, vc, vs_bytes, vs_sc
         gain["c"] = gp
         gain["s"] = gneg
 
-        widen(0, 0, "s")
-        widen(0, 1, "v")
-        widen(1, 0, "v")
-        widen(0, 2, "s")
-        widen(1, 2, "v")
-        transposes(coef_raw[1], 0, "coef", 1)
-        transposes(coef_raw[0], 0, "coef", 0)
-        widen(0, 3, "v")
-        widen(1, 1, "s")
-        widen(1, 3, "v")
-        inter_copy(vsw[0], "vs0", 1, "s")
-        pe_inter(vcr[0], "vc0", 1)
-        transposes_out("coef", 1, "s")
-        pe_inter(vsw[1], "vs1", 0)
+        widen(1, "s")
+        widen(2, "v")
+        transposes("coef", 0)
+        widen(0, "v")
+        widen(3, "v")
+        inter_copy("vs1", 1, "v")
         transposes_out("coef", 0, "s")
-        transposes(u_raw["c", 0], 0, "uc0", 0)
-        inter_copy(vsw[0], "vs0", 0, "v")
-        inter_copy(vsw[1], "vs1", 1, "v")
-        inter_copy(vcr[0], "vc0", 0, "v")
-        quant("vs0", 0, 2)
-        pe_inter_out("vc0", 1, "s")
-        pe_inter_out("vs1", 0, "s")
-        quant("vs0", 1, 2)
-        transposes_out("uc0", 0, "s")
+        inter_copy("vs0", 1, "v")
+        transposes("coef", 1)
+        transposes_out("coef", 1, "s")
+        pe_inter("vs0", 0)
         quant("coef")
-        quant("vc0")
-        quant("vs1")
-        transposes(u_raw["c", 0], 2, "uc0", 1)
-        inter_copy(vcr[1], "vc1", 1, "s")
-        z_mm("s", 0, 0)
-        z_ev("s", 0, 0)
-        z_mm("c", 0, 3)
-        z_ev("c", 0, 3)
-        inter_copy(vcr[1], "vc1", 0, "s")
-        z_mm("s", 0, 1)
-        z_mm("c", 0, 2)
-        z_ev("s", 0, 1)
-        transposes_out("uc0", 1, "s")
-        z_mm("s", 0, 2)
+        pe_inter("vs1", 0)
+        quant("vs0", 1, 2)
+        pe_inter("vc1", 0)
         z_mm("s", 0, 3)
-        z_ev("c", 0, 2)
+        z_mm("s", 0, 2)
+        pe_inter_out("vs0", 0, "s")
+        quant("vs0", 0, 2)
+        pe_inter_out("vs1", 0, "s")
+        z_mm("s", 0, 0)
+        quant("vs1")
+        z_mm("s", 0, 1)
         z_ev("s", 0, 3)
-        transposes(u_raw["s", 0], 0, "us0", 0)
-        transposes_out("us0", 0, "s")
-        transposes(u_raw["s", 0], 2, "us0", 1)
-        z_ev("s", 0, 2)
-        quant("vc1")
-        quant("uc0")
-        z_mm("c", 0, 0)
-        z_ev("c", 0, 0)
-        zp_mm(2)
-        transposes_out("us0", 1, "s")
-        z_mm("c", 0, 1)
-        z_ev("c", 0, 1)
-        zp_mm(3)
-        quant("zs0")
-        quant("us0")
-        zp_mm(1)
-        transposes(u_raw["s", 1], 0, "us1", 0)
-        quant("zc0")
-        transposes(u_raw["s", 1], 2, "us1", 1)
-        zp_ev(2)
-        transposes(u_raw["c", 1], 0, "uc1", 0)
-        zp_ev(3)
-        transposes_out("us1", 0, "s")
-        transposes(u_raw["c", 1], 2, "uc1", 1)
         zp_mm(0)
-        z_mm("c", 1, 1)
-        z_mm("c", 1, 0)
-        zp_ev(1)
-        z_mm("c", 1, 2)
-        transposes_out("us1", 1, "s")
-        quant("us1")
-        transposes_out("uc1", 1, "s")
+        z_ev("s", 0, 0)
+        inter_copy("vc0", 1, "s")
+        pe_inter_out("vc1", 0, "s")
+        zp_mm(3)
+        z_ev("s", 0, 1)
+        transposes("uc0", 0)
+        transposes("uc0", 1)
+        inter_copy("vc0", 0, "s")
+        z_ev("s", 0, 2)
+        quant("vc0")
+        quant("zs0")
+        transposes_out("uc0", 0, "s")
+        transposes("us0", 1)
+        transposes_out("uc0", 1, "s")
+        transposes("us0", 0)
+        z_mm("c", 0, 2)
         zp_ev(0)
-        z_ev("c", 1, 0)
-        z_ev("c", 1, 1)
-        z_ev("c", 1, 2)
-        o_mm(0, 2)
-        pe_inter(zpl, "zs1", 1)
+        zp_ev(3)
+        z_mm("c", 0, 3)
+        inter_copy("vc1", 1, "s")
+        quant("uc0")
+        z_mm("c", 0, 1)
+        z_mm("c", 0, 0)
+        transposes_out("us0", 1, "s")
+        z_ev("c", 0, 2)
+        transposes_out("us0", 0, "s")
+        zp_mm(2)
+        zp_mm(1)
+        transposes("uc1", 1)
+        z_ev("c", 0, 1)
+        transposes_out("uc1", 1, "s")
+        z_ev("c", 0, 0)
+        z_ev("c", 0, 3)
+        transposes("uc1", 0)
+        transposes("us1", 1)
+        quant("vc1")
         transposes_out("uc1", 0, "s")
-        o_ev(0, 2, "s")
-        o_mm(0, 3)
-        o_mm(0, 1)
+        quant("us0")
+        transposes("us1", 0)
+        quant("zc0")
         quant("uc1")
+        zp_ev(1)
+        zp_ev(2)
+        z_mm("c", 1, 0)
+        z_ev("c", 1, 0)
         z_mm("c", 1, 3)
-        pe_inter_out("zs1", 1, "s")
-        o_ev(0, 1, "v")
-        o_mm(0, 0)
-        o_ev(0, 3, "s")
-        o_mm(0, 6)
+        o_mm(0, 2)
+        z_mm("c", 1, 1)
         z_ev("c", 1, 3)
-        o_mm(0, 4)
-        o_mm(0, 7)
-        o_ev(0, 0, "v")
-        quant("zc1")
-        o_ev(0, 4, "v")
-        inter_copy(zpl, "zs1", 0, "s")
+        z_mm("c", 1, 2)
+        z_ev("c", 1, 1)
+        transposes_out("us1", 1, "s")
+        o_ev(0, 2, "s")
+        z_ev("c", 1, 2)
+        transposes_out("us1", 0, "s")
+        quant("us1")
+        o_mm(0, 0)
+        o_mm(0, 3)
+        pe_inter("zs1", 1)
+        o_mm(0, 1)
+        o_ev(0, 3, "v")
+        o_ev(0, 0, "s")
         o_mm(0, 5)
+        o_mm(0, 6)
+        quant("zc1")
+        o_ev(0, 5, "v")
+        o_mm(0, 7)
+        inter_copy("zs1", 0, "s")
+        o_ev(0, 6, "v")
+        o_ev(0, 1, "s")
+        o_mm(0, 4)
+        pe_inter_out("zs1", 1, "s")
         quant("zs1")
         o_mm(1, 5)
-        o_ev(0, 6, "s")
-        o_ev(0, 7, "v")
-        o_ev(0, 5, "v")
-        o_ev(1, 5, "v")
-        o_mm(1, 4)
-        o_ev(1, 4, "v")
         o_mm(1, 6)
+        o_ev(0, 7, "v")
+        o_mm(1, 4)
+        o_ev(0, 4, "v")
         o_mm(1, 0)
+        o_ev(1, 5, "v")
         o_ev(1, 6, "v")
         o_mm(1, 1)
+        o_ev(1, 4, "v")
         o_ev(1, 0, "v")
         o_mm(1, 3)
         o_ev(1, 1, "v")
-        o_mm(1, 2)
         o_ev(1, 3, "v")
-        o_ev(1, 2, "v")
         o_mm(1, 7)
         o_ev(1, 7, "v")
+        o_mm(1, 2)
+        o_ev(1, 2, "v")

@@ -55,24 +55,27 @@ def tile_fourierftgivenbases_kernel(tc, w0, coef, g, uc, us, vc, vs_bytes, vs_sc
         u_raw = {}
         coef_raw = {}
         w0_sb = {}
-        vsb[1] = load("vsb1", [P, 2, F], U8, vsb_v[:, 2 : 4, :])
         vsb[0] = load("vsb0", [P, 2, F], U8, vsb_v[:, 0 : 2, :])
-        coef_raw[0] = load("coef0", [P, 2, N], BF16, coef_v[:, 0 : 2, :])
+        vsb[1] = load("vsb1", [P, 2, F], U8, vsb_v[:, 2 : 4, :])
         coef_raw[1] = load("coef1", [P, 2, N], BF16, coef_v[:, 2 : 4, :])
-        nc.sync.dma_start(out=vcr[:, 0 : 2, :], in_=vc_v[:, 0 : 2, :])
+        coef_raw[0] = load("coef0", [P, 2, N], BF16, coef_v[:, 0 : 2, :])
         nc.sync.dma_start(out=vcr[:, 2 : 4, :], in_=vc_v[:, 2 : 4, :])
-        w0_sb[0] = load("w0_0", [P, 2, F], BF16, w0_v[:, 0 : 2, :])
-        u_raw["c", 0] = load("uc0", [P, 4, N], BF16, u_v["c"][:, 0 : 4, :])
+        nc.sync.dma_start(out=vcr[:, 0 : 2, :], in_=vc_v[:, 0 : 2, :])
         u_raw["s", 0] = load("us0", [P, 4, N], BF16, u_v["s"][:, 0 : 4, :])
+        u_raw["s", 1] = load("us1", [P, 4, N], BF16, u_v["s"][:, 4 : 8, :])
+        u_raw["c", 0] = load("uc0", [P, 4, N], BF16, u_v["c"][:, 0 : 4, :])
         w0_sb[1] = load("w0_1", [P, 2, F], BF16, w0_v[:, 2 : 4, :])
         u_raw["c", 1] = load("uc1", [P, 4, N], BF16, u_v["c"][:, 4 : 8, :])
-        w0_sb[3] = load("w0_3", [P, 2, F], BF16, w0_v[:, 6 : 8, :])
-        u_raw["s", 1] = load("us1", [P, 4, N], BF16, u_v["s"][:, 4 : 8, :])
+        w0_sb[0] = load("w0_0", [P, 2, F], BF16, w0_v[:, 0 : 2, :])
         w0_sb[2] = load("w0_2", [P, 2, F], BF16, w0_v[:, 4 : 6, :])
+        w0_sb[3] = load("w0_3", [P, 2, F], BF16, w0_v[:, 6 : 8, :])
         ident_f = tile("ident_f", [P, P], F32)
-        make_identity(nc, ident_f[:])
+        wz = tile("wz", [P, 512], BF16)
+        nc.vector.memset(wz[:], 0.0)
+        nc.vector.memset(ident_f[:], 0.0)
+        make_identity(nc, ident_f[:], nomemset=True)
         ident_b = tile("ident_b", [P, P], BF16)
-        nc.gpsimd.tensor_copy(out=ident_b[:], in_=ident_f[:])
+        nc.vector.tensor_copy(out=ident_b[:], in_=ident_f[:])
 
         def sc_bank(dt, name):
             return ps.tile([P, 512 if dt == F32 else 1024], dt, name=name, tag="sc", bufs=3)
@@ -235,8 +238,6 @@ def tile_fourierftgivenbases_kernel(tc, w0, coef, g, uc, us, vc, vs_bytes, vs_sc
                 nc.gpsimd.tensor_tensor(out=o[:], in0=half[:], in1=w, op=ADD)
             nc.sync.dma_start(out=out_v[:, i, h * H : (h + 1) * H], in_=o[:])
 
-        wz = tile("wz", [P, 512], BF16)
-        nc.vector.memset(wz[:], 0.0)
         for j in range(NDUMMY):
             wb = sc_bank(F32, "warm%d" % j)
             nc.tensor.matmul(wb[:], wz[:, 0:P], wz[:], start=True, stop=True)
@@ -252,118 +253,118 @@ def tile_fourierftgivenbases_kernel(tc, w0, coef, g, uc, us, vc, vs_bytes, vs_sc
         gain["s"] = gneg
 
         widen(1, "s")
-        widen(2, "v")
-        transposes("coef", 0)
         widen(0, "v")
-        widen(3, "v")
-        inter_copy("vs1", 1, "v")
-        transposes_out("coef", 0, "s")
-        inter_copy("vs0", 1, "v")
         transposes("coef", 1)
+        transposes("coef", 0)
+        widen(2, "v")
+        widen(3, "v")
         transposes_out("coef", 1, "s")
-        pe_inter("vs0", 0)
-        quant("coef")
         pe_inter("vs1", 0)
-        quant("vs0", 1, 2)
-        pe_inter("vc1", 0)
-        z_mm("s", 0, 3)
-        z_mm("s", 0, 2)
-        pe_inter_out("vs0", 0, "s")
-        quant("vs0", 0, 2)
+        transposes_out("coef", 0, "s")
+        pe_inter("vs1", 1)
         pe_inter_out("vs1", 0, "s")
-        z_mm("s", 0, 0)
-        quant("vs1")
+        pe_inter("vc0", 1)
+        inter_copy("vs0", 0, "v")
+        pe_inter_out("vs1", 1, "s")
+        inter_copy("vs0", 1, "v")
+        quant("coef")
+        inter_copy("vc0", 0, "s")
+        pe_inter_out("vc0", 1, "s")
+        quant("vs0", 1, 2)
+        quant("vs0", 0, 2)
+        z_mm("s", 0, 2)
         z_mm("s", 0, 1)
+        z_mm("s", 0, 3)
+        inter_copy("vc1", 0, "v")
+        transposes("us0", 0)
+        quant("vs1")
+        z_ev("s", 0, 1)
+        transposes("us0", 1)
+        transposes_out("us0", 0, "s")
+        zp_mm(3)
+        z_mm("s", 0, 0)
+        transposes_out("us0", 1, "s")
+        quant("vc0")
+        transposes("us1", 0)
+        zp_ev(3)
+        z_ev("s", 0, 2)
+        z_mm("c", 0, 1)
         z_ev("s", 0, 3)
         zp_mm(0)
         z_ev("s", 0, 0)
-        inter_copy("vc0", 1, "s")
-        pe_inter_out("vc1", 0, "s")
-        zp_mm(3)
-        z_ev("s", 0, 1)
+        z_mm("c", 0, 0)
+        inter_copy("vc1", 1, "s")
+        quant("us0")
+        z_ev("c", 0, 1)
+        z_mm("c", 0, 3)
+        transposes_out("us1", 0, "s")
+        zp_ev(0)
+        z_mm("c", 0, 2)
         transposes("uc0", 0)
         transposes("uc0", 1)
-        inter_copy("vc0", 0, "s")
-        z_ev("s", 0, 2)
-        quant("vc0")
-        quant("zs0")
-        transposes_out("uc0", 0, "s")
-        transposes("us0", 1)
-        transposes_out("uc0", 1, "s")
-        transposes("us0", 0)
-        z_mm("c", 0, 2)
-        zp_ev(0)
-        zp_ev(3)
-        z_mm("c", 0, 3)
-        inter_copy("vc1", 1, "s")
-        quant("uc0")
-        z_mm("c", 0, 1)
-        z_mm("c", 0, 0)
-        transposes_out("us0", 1, "s")
-        z_ev("c", 0, 2)
-        transposes_out("us0", 0, "s")
         zp_mm(2)
-        zp_mm(1)
-        transposes("uc1", 1)
-        z_ev("c", 0, 1)
-        transposes_out("uc1", 1, "s")
-        z_ev("c", 0, 0)
-        z_ev("c", 0, 3)
-        transposes("uc1", 0)
-        transposes("us1", 1)
         quant("vc1")
-        transposes_out("uc1", 0, "s")
-        quant("us0")
-        transposes("us1", 0)
-        quant("zc0")
-        quant("uc1")
-        zp_ev(1)
-        zp_ev(2)
-        z_mm("c", 1, 0)
-        z_ev("c", 1, 0)
-        z_mm("c", 1, 3)
-        o_mm(0, 2)
+        zp_mm(1)
+        z_ev("c", 0, 3)
+        transposes_out("uc0", 0, "s")
+        z_ev("c", 0, 0)
+        transposes("uc1", 1)
         z_mm("c", 1, 1)
-        z_ev("c", 1, 3)
+        transposes_out("uc0", 1, "s")
+        zp_ev(2)
+        z_ev("c", 0, 2)
         z_mm("c", 1, 2)
+        quant("zs0")
+        quant("uc0")
+        z_mm("c", 1, 0)
+        transposes("us1", 1)
+        zp_ev(1)
+        transposes_out("uc1", 1, "s")
+        quant("zc0")
+        transposes("uc1", 0)
+        o_mm(0, 2)
         z_ev("c", 1, 1)
-        transposes_out("us1", 1, "s")
-        o_ev(0, 2, "s")
         z_ev("c", 1, 2)
-        transposes_out("us1", 0, "s")
+        transposes_out("us1", 1, "s")
         quant("us1")
-        o_mm(0, 0)
+        pe_inter("zs1", 0)
+        transposes_out("uc1", 0, "s")
+        o_ev(0, 2, "s")
         o_mm(0, 3)
-        pe_inter("zs1", 1)
-        o_mm(0, 1)
-        o_ev(0, 3, "v")
-        o_ev(0, 0, "s")
+        z_mm("c", 1, 3)
+        pe_inter_out("zs1", 0, "s")
+        quant("uc1")
         o_mm(0, 5)
+        z_ev("c", 1, 0)
+        z_ev("c", 1, 3)
+        o_ev(0, 5, "v")
         o_mm(0, 6)
         quant("zc1")
-        o_ev(0, 5, "v")
-        o_mm(0, 7)
-        inter_copy("zs1", 0, "s")
-        o_ev(0, 6, "v")
-        o_ev(0, 1, "s")
+        o_mm(0, 1)
+        o_ev(0, 3, "s")
+        o_ev(0, 1, "v")
         o_mm(0, 4)
-        pe_inter_out("zs1", 1, "s")
-        quant("zs1")
-        o_mm(1, 5)
-        o_mm(1, 6)
-        o_ev(0, 7, "v")
-        o_mm(1, 4)
         o_ev(0, 4, "v")
-        o_mm(1, 0)
-        o_ev(1, 5, "v")
-        o_ev(1, 6, "v")
-        o_mm(1, 1)
-        o_ev(1, 4, "v")
-        o_ev(1, 0, "v")
-        o_mm(1, 3)
-        o_ev(1, 1, "v")
-        o_ev(1, 3, "v")
-        o_mm(1, 7)
-        o_ev(1, 7, "v")
+        o_mm(0, 0)
+        inter_copy("zs1", 1, "s")
+        quant("zs1")
+        o_mm(0, 7)
+        o_ev(0, 6, "s")
+        o_ev(0, 7, "v")
+        o_ev(0, 0, "v")
         o_mm(1, 2)
+        o_mm(1, 1)
         o_ev(1, 2, "v")
+        o_mm(1, 0)
+        o_mm(1, 6)
+        o_ev(1, 1, "v")
+        o_ev(1, 0, "v")
+        o_mm(1, 4)
+        o_ev(1, 6, "v")
+        o_ev(1, 4, "v")
+        o_mm(1, 3)
+        o_mm(1, 7)
+        o_ev(1, 3, "v")
+        o_mm(1, 5)
+        o_ev(1, 7, "v")
+        o_ev(1, 5, "v")

from contextlib import ExitStack

import concourse.mybir as mybir
from concourse.masks import make_identity

D, F, N = 1024, 1024, 512
FLOPS = 2 * 2 * N * N * F + 2 * 2 * D * N * F

F32 = mybir.dt.float32
BF16 = mybir.dt.bfloat16
U32 = mybir.dt.uint32
U8 = mybir.dt.uint8
FP8 = mybir.dt.float8_e4m3fn
FP8X4 = mybir.dt.float8_e4m3fn_x4
MULT = mybir.AluOpType.mult
ADD = mybir.AluOpType.add
COPY = mybir.ActivationFunctionType.Copy

P = 128
T = 4
H = 512
I = 8
NDUMMY = 8


def tile_fourierftgivenbases_kernel(tc, w0, coef, g, uc, us, vc, vs_bytes, vs_scale, out):
    nc = tc.nc
    with ExitStack() as ctx:
        sb = ctx.enter_context(tc.tile_pool(name="sb", bufs=1))
        ps = ctx.enter_context(tc.psum_pool(name="ps", bufs=1))
        ctx.enter_context(tc.manual_schedule())

        def tile(name, shape, dt):
            return sb.tile(shape, dt, name=name, align_bytes=64)

        def load(name, shape, dt, src):
            t = tile(name, shape, dt)
            nc.sync.dma_start(out=t[:], in_=src)
            return t

        vsb_v = vs_bytes.rearrange("(p t) f -> p t f", t=T)
        vc_v = vc.rearrange("(p t) f -> p t f", t=T)
        coef_v = coef.rearrange("(p t) k -> p t k", t=T)
        u_v = {"c": uc.rearrange("(p i) n -> p i n", i=I), "s": us.rearrange("(p i) n -> p i n", i=I)}
        w0_v = w0.rearrange("(p i) f -> p i f", i=I)
        out_v = out.rearrange("(p i) f -> p i f", i=I)

        vscale = tile("vscale", [P, T], F32)
        nc.scalar.dma_start(out=vscale[:], in_=vs_scale.rearrange("(p t) o -> p (t o)", t=T))
        gp = tile("gp", [P, T], BF16)
        nc.scalar.dma_start(out=gp[:], in_=g.rearrange("(p t) -> p t", t=T))

        vsb = {}
        vcr = tile("vcr", [P, T, F], BF16)
        u_raw = {}
        coef_raw = {}
        w0_sb = {}
        vsb[0] = load("vsb0", [P, 2, F], U8, vsb_v[:, 0 : 2, :])
        vsb[1] = load("vsb1", [P, 2, F], U8, vsb_v[:, 2 : 4, :])
        coef_raw[1] = load("coef1", [P, 2, N], BF16, coef_v[:, 2 : 4, :])
        coef_raw[0] = load("coef0", [P, 2, N], BF16, coef_v[:, 0 : 2, :])
        nc.sync.dma_start(out=vcr[:, 2 : 4, :], in_=vc_v[:, 2 : 4, :])
        nc.sync.dma_start(out=vcr[:, 0 : 2, :], in_=vc_v[:, 0 : 2, :])
        u_raw["s", 0] = load("us0", [P, 4, N], BF16, u_v["s"][:, 0 : 4, :])
        u_raw["s", 1] = load("us1", [P, 4, N], BF16, u_v["s"][:, 4 : 8, :])
        u_raw["c", 0] = load("uc0", [P, 4, N], BF16, u_v["c"][:, 0 : 4, :])
        w0_sb[1] = load("w0_1", [P, 2, F], BF16, w0_v[:, 2 : 4, :])
        u_raw["c", 1] = load("uc1", [P, 4, N], BF16, u_v["c"][:, 4 : 8, :])
        w0_sb[0] = load("w0_0", [P, 2, F], BF16, w0_v[:, 0 : 2, :])
        w0_sb[2] = load("w0_2", [P, 2, F], BF16, w0_v[:, 4 : 6, :])
        w0_sb[3] = load("w0_3", [P, 2, F], BF16, w0_v[:, 6 : 8, :])
        ident_f = tile("ident_f", [P, P], F32)
        wz = tile("wz", [P, 512], BF16)
        nc.vector.memset(wz[:], 0.0)
        nc.vector.memset(ident_f[:], 0.0)
        make_identity(nc, ident_f[:], nomemset=True)
        ident_b = tile("ident_b", [P, P], BF16)
        nc.vector.tensor_copy(out=ident_b[:], in_=ident_f[:])

        def sc_bank(dt, name):
            return ps.tile([P, 512 if dt == F32 else 1024], dt, name=name, tag="sc", bufs=3)

        def zo_bank(name):
            return ps.tile([P, 512], F32, name=name, tag="zo", bufs=5)

        codes = {}
        scales = {}
        inter = {}
        sbank = {}

        def new_inter(key, cols=512):
            inter[key] = tile("in_" + key, [P, cols * T], BF16)

        def quant(key, part=0, parts=1):
            if key not in codes:
                codes[key] = tile("co_" + key, [P, 512], U32)
                scales[key] = tile("sl_" + key, [P, 512], U8)
            cols = slice(part * 512 // parts, (part + 1) * 512 // parts)
            ins = slice(part * 2048 // parts, (part + 1) * 2048 // parts)
            nc.vector.quantize_mx(out=codes[key][:, cols].bitcast(FP8X4), scales=scales[key][:, cols], in_=inter[key][:, ins])

        def mx(dst, lkey, l0, rkey, r0, n, start, stop):
            nc.tensor.matmul_mx(
                out=dst,
                lhsT=codes[lkey][:, l0 : l0 + P].bitcast(FP8X4),
                lhsT_scale=scales[lkey][:, l0 : l0 + P],
                rhs=codes[rkey][:, r0 : r0 + n].bitcast(FP8X4),
                rhs_scale=scales[rkey][:, r0 : r0 + n],
                start=start,
                stop=stop,
            )

        def transposes(key, half):
            raw, first = (coef_raw[half], 0) if key == "coef" else (u_raw[key[1], int(key[2])], 2 * half)
            bank = sc_bank(F32, "tr_%s%d" % (key, half))
            sbank[key, half] = bank
            for i in range(2):
                words = raw[:, first + i, :].bitcast(F32)
                for u in range(2):
                    nc.tensor.transpose(bank[:, (2 * i + u) * P : (2 * i + u + 1) * P], words[:, u::2], ident_f[:])

        def transposes_out(key, half, eng):
            bank = sbank[key, half]
            copy = nc.scalar.copy if eng == "s" else nc.vector.tensor_copy
            dst = inter[key][:].bitcast(F32)[:, half * 512 : (half + 1) * 512]
            copy(
                out=dst.rearrange("p (i r u) -> p i r u", i=2, u=2),
                in_=bank[:].rearrange("p (i u r) -> p i r u", i=2, u=2),
            )

        def planes_of(key):
            if key == "zs1":
                return zpl
            h = int(key[2])
            return (vsw if key[1] == "s" else vcr)[:, :, h * H : (h + 1) * H]

        def pe_inter(key, half):
            planes = planes_of(key)
            bank = sc_bank(BF16, "il_%s%d" % (key, half))
            sbank[key, half] = bank
            for b in range(2):
                f0 = half * 256 + b * 128
                nc.tensor.matmul(
                    bank[:, b * 512 : (b + 1) * 512],
                    ident_b[:],
                    planes[:, :, f0 : f0 + 128].rearrange("p t f -> p f t"),
                    start=True,
                    stop=True,
                )

        def pe_inter_out(key, half, eng):
            copy = nc.scalar.copy if eng == "s" else nc.vector.tensor_copy
            copy(out=inter[key][:, half * 1024 : (half + 1) * 1024], in_=sbank[key, half][:])

        def inter_copy(key, half, eng):
            planes = planes_of(key)
            copy = nc.scalar.copy if eng == "s" else nc.vector.tensor_copy
            copy(
                out=inter[key][:, half * 1024 : (half + 1) * 1024].rearrange("p (c i t) -> p c t i", t=T, i=4),
                in_=planes[:, :, half * 256 : (half + 1) * 256].rearrange("p t (c i) -> p c t i", i=4),
            )

        vsw = tile("vsw", [P, T, F], BF16)

        def widen(t, eng):
            src = vsb[t // 2][:, t % 2, :].bitcast(FP8)
            if eng == "v":
                nc.vector.tensor_scalar(out=vsw[:, t, :], in0=src, scalar1=vscale[:, t : t + 1], scalar2=None, op0=MULT)
            else:
                nc.scalar.activation(out=vsw[:, t, :], in_=src, func=COPY, scale=vscale[:, t : t + 1])

        zbank = {}

        def z_mm(o, h, q):
            bank = zo_bank("z%s%d%d" % (o, h, q))
            for t in range(T):
                mx(bank[:, t * P : (t + 1) * P], "coef", t * P, "v%s%d" % (o, h), q * P, P, True, True)
            zbank[o, h, q] = bank

        gain = {}
        zpl = tile("zpl", [P, T, H], BF16)

        def zp_mm(t):
            bank = zo_bank("zp%d" % t)
            mx(bank[:], "coef", t * P, "vs1", 0, H, True, True)
            zbank["p", t] = bank

        def zp_ev(t):
            nc.scalar.activation(out=zpl[:, t, :], in_=zbank["p", t][:], func=COPY, scale=gneg32[:, t : t + 1])

        def z_ev(o, h, q):
            nc.vector.tensor_tensor(
                out=inter["z%s%d" % (o, h)][:, q * 512 : (q + 1) * 512].rearrange("p (n t) -> p n t", t=T),
                in0=zbank[o, h, q][:].rearrange("p (t n) -> p n t", t=T),
                in1=gain[o][:].unsqueeze(1).to_broadcast([P, P, T]),
                op=MULT,
            )

        def o2_mm(c, j):
            bank = zo_bank("q%d%d" % (c, j))
            for e in range(2):
                l0 = ((2 * j + e) % 4) * P
                mx(bank[:, e * 256 : (e + 1) * 256], "uc%d" % (j // 2), l0, "zc1", c * 256, 256, True, False)
                mx(bank[:, e * 256 : (e + 1) * 256], "us%d" % (j // 2), l0, "zs1", c * 256, 256, False, True)
            obank["ab"[c], j] = bank

        def o2_ev(c, j, eng):
            bank = obank["ab"[c], j][:].rearrange("p (e f) -> p e f", e=2)
            f0 = H + c * 256
            w = w0_sb[j][:, :, f0 : f0 + 256]
            o = tile("ou%d%d" % (c, j), [P, 2, 256], F32)
            if eng == "v":
                nc.vector.scalar_tensor_tensor(out=o[:], in0=bank, scalar=0.5, in1=w, op0=MULT, op1=ADD)
            else:
                half = tile("og%d%d" % (c, j), [P, 2, 256], F32)
                nc.scalar.activation(out=half[:], in_=bank, func=COPY, scale=0.5)
                nc.gpsimd.tensor_tensor(out=o[:], in0=half[:], in1=w, op=ADD)
            nc.sync.dma_start(out=out_v[:, 2 * j : 2 * j + 2, f0 : f0 + 256], in_=o[:])

        obank = {}

        def o_mm(h, i):
            bank = zo_bank("o%d%d" % (h, i))
            l0 = (i % 4) * P
            mx(bank[:], "uc%d" % (i // 4), l0, "zc%d" % h, 0, H, True, False)
            mx(bank[:], "us%d" % (i // 4), l0, "zs%d" % h, 0, H, False, True)
            obank[h, i] = bank

        def o_ev(h, i, eng):
            bank = obank[h, i]
            w = w0_sb[i // 2][:, i % 2, h * H : (h + 1) * H]
            o = tile("ot%d%d" % (h, i), [P, H], F32)
            if eng == "v":
                nc.vector.scalar_tensor_tensor(out=o[:], in0=bank[:], scalar=0.5, in1=w, op0=MULT, op1=ADD)
            else:
                half = tile("oh%d%d" % (h, i), [P, H], F32)
                nc.scalar.activation(out=half[:], in_=bank[:], func=COPY, scale=0.5)
                nc.gpsimd.tensor_tensor(out=o[:], in0=half[:], in1=w, op=ADD)
            nc.sync.dma_start(out=out_v[:, i, h * H : (h + 1) * H], in_=o[:])

        for j in range(NDUMMY):
            wb = sc_bank(F32, "warm%d" % j)
            nc.tensor.matmul(wb[:], wz[:, 0:P], wz[:], start=True, stop=True)

        for k in ("coef", "vc0", "vc1", "vs0", "vs1", "zc0", "zc1", "zs0", "zs1", "uc0", "uc1", "us0", "us1"):
            new_inter(k)

        gneg = tile("gneg", [P, T], BF16)
        nc.gpsimd.tensor_scalar(out=gneg[:], in0=gp[:], scalar1=-1.0, scalar2=None, op0=MULT)
        gneg32 = tile("gneg32", [P, T], F32)
        nc.gpsimd.tensor_scalar(out=gneg32[:], in0=gp[:], scalar1=-1.0, scalar2=None, op0=MULT)
        gain["c"] = gp
        gain["s"] = gneg

        widen(1, "s")
        widen(0, "v")
        transposes("coef", 1)
        transposes("coef", 0)
        widen(2, "v")
        widen(3, "v")
        transposes_out("coef", 1, "s")
        pe_inter("vs1", 0)
        transposes_out("coef", 0, "s")
        pe_inter("vs1", 1)
        pe_inter_out("vs1", 0, "s")
        pe_inter("vc0", 1)
        inter_copy("vs0", 0, "v")
        pe_inter_out("vs1", 1, "s")
        inter_copy("vs0", 1, "v")
        quant("coef")
        inter_copy("vc0", 0, "s")
        pe_inter_out("vc0", 1, "s")
        quant("vs0", 1, 2)
        quant("vs0", 0, 2)
        z_mm("s", 0, 2)
        z_mm("s", 0, 1)
        z_mm("s", 0, 3)
        inter_copy("vc1", 0, "v")
        transposes("us0", 0)
        quant("vs1")
        z_ev("s", 0, 1)
        transposes("us0", 1)
        transposes_out("us0", 0, "s")
        zp_mm(3)
        z_mm("s", 0, 0)
        transposes_out("us0", 1, "s")
        quant("vc0")
        transposes("us1", 0)
        zp_ev(3)
        z_ev("s", 0, 2)
        z_mm("c", 0, 1)
        z_ev("s", 0, 3)
        zp_mm(0)
        z_ev("s", 0, 0)
        z_mm("c", 0, 0)
        inter_copy("vc1", 1, "s")
        quant("us0")
        z_ev("c", 0, 1)
        z_mm("c", 0, 3)
        transposes_out("us1", 0, "s")
        zp_ev(0)
        z_mm("c", 0, 2)
        transposes("uc0", 0)
        transposes("uc0", 1)
        zp_mm(2)
        quant("vc1")
        zp_mm(1)
        z_ev("c", 0, 3)
        transposes_out("uc0", 0, "s")
        z_ev("c", 0, 0)
        transposes("uc1", 1)
        z_mm("c", 1, 1)
        transposes_out("uc0", 1, "s")
        zp_ev(2)
        z_ev("c", 0, 2)
        z_mm("c", 1, 2)
        quant("zs0")
        quant("uc0")
        z_mm("c", 1, 0)
        transposes("us1", 1)
        zp_ev(1)
        transposes_out("uc1", 1, "s")
        quant("zc0")
        transposes("uc1", 0)
        o_mm(0, 2)
        z_ev("c", 1, 1)
        z_ev("c", 1, 2)
        transposes_out("us1", 1, "s")
        quant("us1")
        pe_inter("zs1", 0)
        transposes_out("uc1", 0, "s")
        o_ev(0, 2, "s")
        o_mm(0, 3)
        z_mm("c", 1, 3)
        pe_inter_out("zs1", 0, "s")
        quant("uc1")
        o_mm(0, 5)
        z_ev("c", 1, 0)
        z_ev("c", 1, 3)
        o_ev(0, 5, "v")
        o_mm(0, 6)
        quant("zc1")
        o_mm(0, 1)
        o_ev(0, 3, "s")
        o_ev(0, 1, "v")
        o_mm(0, 4)
        o_ev(0, 4, "v")
        o_mm(0, 0)
        inter_copy("zs1", 1, "s")
        quant("zs1")
        o_mm(0, 7)
        o_ev(0, 6, "s")
        o_ev(0, 7, "v")
        o_ev(0, 0, "v")
        o_mm(1, 2)
        o_mm(1, 1)
        o_ev(1, 2, "v")
        o_mm(1, 0)
        o_mm(1, 6)
        o_ev(1, 1, "v")
        o_ev(1, 0, "v")
        o_mm(1, 4)
        o_ev(1, 6, "v")
        o_ev(1, 4, "v")
        o_mm(1, 3)
        o_mm(1, 7)
        o_ev(1, 3, "v")
        o_mm(1, 5)
        o_ev(1, 7, "v")
        o_ev(1, 5, "v")
